import numpy as np
import ml_dtypes


def mxq(x, axis, fmt="e4m3"):
    dtype, down = {"e4m3": (ml_dtypes.float8_e4m3fn, 7), "e5m2": (ml_dtypes.float8_e5m2, 14)}[fmt]
    v = np.moveaxis(np.asarray(x, np.float32).astype(ml_dtypes.bfloat16).astype(np.float64), axis, -1)
    blocks = v.reshape(v.shape[:-1] + (-1, 32))
    amax = np.abs(blocks).max(-1, keepdims=True)
    byte = np.maximum(np.where(amax > 0, np.frexp(amax)[1] - 1 + 127, 0) - down, 1)
    scale = np.exp2(byte - 127.0)
    codes = (blocks / scale).astype(np.float32).astype(dtype).astype(np.float64)
    return np.moveaxis((codes * scale).reshape(v.shape), -1, axis)


WIDE = False


def mx_kscale(k, group=512):
    if not WIDE:
        return np.ones(k)
    levels = np.array([18, -18])
    if group != 512:
        return np.exp2(np.random.permutation(np.resize(levels, k // group))).repeat(group)
    if k % 512:
        return np.exp2(np.random.permutation(np.resize(levels, k // 32))).repeat(32)
    a = np.empty((k // 512, 16))
    for p in range(k // 512):
        a[p, :8] = np.random.permutation(np.resize(levels, 8))
        for g in range(8):
            far = levels[np.abs(levels - a[p, g]) >= 10]
            a[p, g + 8] = far[np.random.randint(len(far))]
    return np.exp2(a.ravel()).repeat(32)


def f64(x):
    return np.asarray(x).astype(np.float64)


G, D, M, N = 4, 128, 128, 512


def setup_inputs():
    n = np.random.standard_normal
    s = mx_kscale(D, 0)[:, None]
    return {
        "x": (n((G, D, N)) * s).astype(np.float32),
        "w": (n((G, D, M)) / np.sqrt(D) / s).astype(np.float32),
        "u": (n((G, D, M)) / np.sqrt(D) / s).astype(np.float32),
        "b": (0.5 * n((G, M, 1))).astype(np.float32),
    }


def reference(x, w, u, b):
    xq = mxq(f64(x), 1, "e4m3")
    h = mxq(f64(w), 1, "e4m3").transpose(0, 2, 1) @ xq
    g = mxq(f64(u), 1, "e4m3").transpose(0, 2, 1) @ xq
    h = h + f64(b)
    y = np.maximum(h, 0.0) * g
    return y

@@ -1,0 +1,115 @@
+from contextlib import ExitStack
+
+import concourse.mybir as mybir
+
+G, D, M, N = 4, 128, 128, 512
+FLOPS = 2 * 2 * G * D * M * N
+
+F32 = mybir.dt.float32
+BF16 = mybir.dt.bfloat16
+U32 = mybir.dt.uint32
+U8 = mybir.dt.uint8
+FP8X4 = mybir.dt.float8_e4m3fn_x4
+RELU = mybir.ActivationFunctionType.Relu
+MULT = mybir.AluOpType.mult
+
+P = 128
+PACK = 4
+ROWS = D // PACK
+UNIT = 128
+
+
+def tile_rows_gglu_relu_bias_kernel(tc, x, w, u, b, out):
+    nc = tc.nc
+    with ExitStack() as ctx:
+        sb = ctx.enter_context(tc.tile_pool(name="sb", bufs=1))
+        ps = ctx.enter_context(tc.psum_pool(name="ps", bufs=1))
+        ctx.enter_context(tc.manual_schedule())
+
+        x_rows = x.rearrange("g (p j) n -> (g p) j n", j=PACK)
+        w_rows = w.rearrange("g (p j) m -> (g p) j m", j=PACK)
+        u_rows = u.rearrange("g (p j) m -> (g p) j m", j=PACK)
+
+        bias_rows = sb.tile([P, P], F32, name="bias_rows", align_bytes=64)
+        bias_cols = sb.tile([P, P], F32, name="bias_cols", align_bytes=64)
+        w_raw = sb.tile([P, PACK, M], F32, name="w_raw")
+        u_raw = sb.tile([P, PACK, M], F32, name="u_raw")
+        x_codes = sb.tile([P, N], U32, name="x_codes", align_bytes=64)
+        x_scales = sb.tile([P, N], U8, name="x_scales", align_bytes=64)
+        w_codes = sb.tile([P, M], U32, name="w_codes", align_bytes=64)
+        w_scales = sb.tile([P, M], U8, name="w_scales", align_bytes=64)
+        u_codes = sb.tile([P, M], U32, name="u_codes", align_bytes=64)
+        u_scales = sb.tile([P, M], U8, name="u_scales", align_bytes=64)
+
+        nc.vector.memset(bias_rows[:], 0.0)
+        nc.scalar.dma_start(
+            out=bias_rows[0:P:32, :].rearrange("q (g j) -> q g j", j=32),
+            in_=b.rearrange("g (q j) o -> q g (j o)", j=32),
+        )
+        x_raw = sb.tile([P, PACK, N], F32, name="x_raw")
+        nc.sync.dma_start(out=x_raw[:], in_=x_rows)
+        nc.sync.dma_start(out=w_raw[:], in_=w_rows)
+        nc.sync.dma_start(out=u_raw[:], in_=u_rows)
+
+        def x_unit(i):
+            return x_raw[:, :, i * UNIT : (i + 1) * UNIT]
+
+        raw = {"w": w_raw[:], "u": u_raw[:]}
+        codes = {"w": w_codes[:], "u": u_codes[:]}
+        scales = {"w": w_scales[:], "u": u_scales[:]}
+        for i in range(N // UNIT):
+            raw["x%d" % i] = x_unit(i)
+            codes["x%d" % i] = x_codes[:, i * UNIT : (i + 1) * UNIT]
+            scales["x%d" % i] = x_scales[:, i * UNIT : (i + 1) * UNIT]
+        packed = {}
+
+        def interleave(key, copy):
+            packed[key] = sb.tile([P, UNIT, PACK], BF16, name="packed_" + key, align_bytes=64)
+            copy(
+                out=packed[key][:].rearrange("p (c i) t -> p c t i", i=4),
+                in_=raw[key].rearrange("p t (c i) -> p c t i", i=4),
+            )
+
+        def quantize(key):
+            nc.vector.quantize_mx(
+                out=codes[key].bitcast(FP8X4),
+                scales=scales[key],
+                in_=packed[key][:].rearrange("p n t -> p (n t)"),
+            )
+
+        def product(g, name, w_c, w_s):
+            rows = slice(g * ROWS, (g + 1) * ROWS)
+            acc = ps.tile([M, N], F32, name="%s%d" % (name, g))
+            nc.tensor.matmul_mx(
+                out=acc[:],
+                lhsT=w_c[rows, :].bitcast(FP8X4),
+                lhsT_scale=w_s[rows, :],
+                rhs=x_codes[rows, :].bitcast(FP8X4),
+                rhs_scale=x_scales[rows, :],
+                start=True,
+                stop=True,
+            )
+            return acc
+
+        nc.vector.transpose(out=bias_cols[:], in_=bias_rows[:])
+        interleave("x0", nc.vector.tensor_copy)
+        interleave("x2", nc.scalar.copy)
+        interleave("x1", nc.vector.tensor_copy)
+        interleave("x3", nc.scalar.copy)
+        interleave("w", nc.vector.tensor_copy)
+        interleave("u", nc.scalar.copy)
+        quantize("x0")
+        quantize("x1")
+        quantize("x2")
+        quantize("w")
+        quantize("x3")
+        quantize("u")
+
+        z = [product(g, "z", w_codes, w_scales) for g in range(G)]
+        gate = [product(g, "gate", u_codes, u_scales) for g in range(G)]
+        for g in range(G):
+            act = sb.tile([M, N], F32, name="act%d" % g)
+            nc.scalar.activation(out=act[:], in_=z[g][:], func=RELU, bias=bias_cols[:, 32 * g : 32 * g + 1])
+            res = sb.tile([M, N], F32, name="res%d" % g)
+            nc.vector.tensor_tensor(out=res[:], in0=gate[g][:], in1=act[:], op=MULT)
+            nc.sync.dma_start(out=out[g], in_=res[:])

@@ -46,13 +46,14 @@ def tile_rows_gglu_relu_bias_kernel(tc, x, w, u, b, out):
             out=bias_rows[0:P:32, :].rearrange("q (g j) -> q g j", j=32),
             in_=b.rearrange("g (q j) o -> q g (j o)", j=32),
         )
-        x_raw = sb.tile([P, PACK, N], F32, name="x_raw")
-        nc.sync.dma_start(out=x_raw[:], in_=x_rows)
+        x_raw = [sb.tile([P, PACK, N // 2], F32, name="x_raw%d" % h) for h in range(2)]
+        nc.sync.dma_start(out=x_raw[0][:], in_=x_rows[:, :, : N // 2])
         nc.sync.dma_start(out=w_raw[:], in_=w_rows)
+        nc.sync.dma_start(out=x_raw[1][:], in_=x_rows[:, :, N // 2 :])
         nc.sync.dma_start(out=u_raw[:], in_=u_rows)
 
         def x_unit(i):
-            return x_raw[:, :, i * UNIT : (i + 1) * UNIT]
+            return x_raw[i // 2][:, :, (i % 2) * UNIT : (i % 2 + 1) * UNIT]
 
         raw = {"w": w_raw[:], "u": u_raw[:]}
         codes = {"w": w_codes[:], "u": u_codes[:]}
@@ -91,18 +92,18 @@ def tile_rows_gglu_relu_bias_kernel(tc, x, w, u, b, out):
             )
             return acc
 
-        nc.vector.transpose(out=bias_cols[:], in_=bias_rows[:])
         interleave("x0", nc.vector.tensor_copy)
-        interleave("x2", nc.scalar.copy)
-        interleave("x1", nc.vector.tensor_copy)
-        interleave("x3", nc.scalar.copy)
+        interleave("x1", nc.scalar.copy)
         interleave("w", nc.vector.tensor_copy)
-        interleave("u", nc.scalar.copy)
         quantize("x0")
         quantize("x1")
-        quantize("x2")
         quantize("w")
+        interleave("x2", nc.vector.tensor_copy)
+        interleave("x3", nc.scalar.copy)
+        interleave("u", nc.scalar.copy)
+        quantize("x2")
         quantize("x3")
+        nc.vector.transpose(out=bias_cols[:], in_=bias_rows[:])
         quantize("u")
 
         z = [product(g, "z", w_codes, w_scales) for g in range(G)]
@@ -110,6 +111,10 @@ def tile_rows_gglu_relu_bias_kernel(tc, x, w, u, b, out):
         for g in range(G):
             act = sb.tile([M, N], F32, name="act%d" % g)
             nc.scalar.activation(out=act[:], in_=z[g][:], func=RELU, bias=bias_cols[:, 32 * g : 32 * g + 1])
-            res = sb.tile([M, N], F32, name="res%d" % g)
-            nc.vector.tensor_tensor(out=res[:], in0=gate[g][:], in1=act[:], op=MULT)
-            nc.sync.dma_start(out=out[g], in_=res[:])
+            pieces = 2 if g == G - 1 else 1
+            width = N // pieces
+            for k in range(pieces):
+                cols = slice(k * width, (k + 1) * width)
+                res = sb.tile([M, width], F32, name="res%d_%d" % (g, k))
+                nc.vector.tensor_tensor(out=res[:], in0=gate[g][:, cols], in1=act[:, cols], op=MULT)
+                nc.sync.dma_start(out=out[g][:, cols], in_=res[:])

@@ -48,8 +48,8 @@ def tile_rows_gglu_relu_bias_kernel(tc, x, w, u, b, out):
         )
         x_raw = [sb.tile([P, PACK, N // 2], F32, name="x_raw%d" % h) for h in range(2)]
         nc.sync.dma_start(out=x_raw[0][:], in_=x_rows[:, :, : N // 2])
-        nc.sync.dma_start(out=w_raw[:], in_=w_rows)
         nc.sync.dma_start(out=x_raw[1][:], in_=x_rows[:, :, N // 2 :])
+        nc.sync.dma_start(out=w_raw[:], in_=w_rows)
         nc.sync.dma_start(out=u_raw[:], in_=u_rows)
 
         def x_unit(i):
@@ -94,27 +94,35 @@ def tile_rows_gglu_relu_bias_kernel(tc, x, w, u, b, out):
 
         interleave("x0", nc.vector.tensor_copy)
         interleave("x1", nc.scalar.copy)
-        interleave("w", nc.vector.tensor_copy)
         quantize("x0")
         quantize("x1")
-        quantize("w")
         interleave("x2", nc.vector.tensor_copy)
         interleave("x3", nc.scalar.copy)
-        interleave("u", nc.scalar.copy)
+        interleave("w", nc.vector.tensor_copy)
         quantize("x2")
         quantize("x3")
+        quantize("w")
+        interleave("u", nc.scalar.copy)
         nc.vector.transpose(out=bias_cols[:], in_=bias_rows[:])
         quantize("u")
 
-        z = [product(g, "z", w_codes, w_scales) for g in range(G)]
-        gate = [product(g, "gate", u_codes, u_scales) for g in range(G)]
+        z, gate = {}, {}
+        z[0] = product(0, "z", w_codes, w_scales)
+        z[1] = product(1, "z", w_codes, w_scales)
+        gate[0] = product(0, "gate", u_codes, u_scales)
+        z[2] = product(2, "z", w_codes, w_scales)
+        gate[1] = product(1, "gate", u_codes, u_scales)
+        z[3] = product(3, "z", w_codes, w_scales)
+        gate[2] = product(2, "gate", u_codes, u_scales)
+        gate[3] = product(3, "gate", u_codes, u_scales)
+        half = N // 2
         for g in range(G):
-            act = sb.tile([M, N], F32, name="act%d" % g)
-            nc.scalar.activation(out=act[:], in_=z[g][:], func=RELU, bias=bias_cols[:, 32 * g : 32 * g + 1])
-            pieces = 2 if g == G - 1 else 1
-            width = N // pieces
-            for k in range(pieces):
-                cols = slice(k * width, (k + 1) * width)
-                res = sb.tile([M, width], F32, name="res%d_%d" % (g, k))
-                nc.vector.tensor_tensor(out=res[:], in0=gate[g][:, cols], in1=act[:, cols], op=MULT)
+            for k in range(2):
+                cols = slice(k * half, (k + 1) * half)
+                act = sb.tile([M, half], F32, name="act%d_%d" % (g, k))
+                nc.scalar.activation(
+                    out=act[:], in_=z[g][:, cols], func=RELU, bias=bias_cols[:, 32 * g : 32 * g + 1]
+                )
+                res = sb.tile([M, half], F32, name="res%d_%d" % (g, k))
+                nc.vector.tensor_tensor(out=res[:], in0=gate[g][:, cols], in1=act[:], op=MULT)
                 nc.sync.dma_start(out=out[g][:, cols], in_=res[:])

@@ -36,8 +36,8 @@ def tile_rows_gglu_relu_bias_kernel(tc, x, w, u, b, out):
         u_raw = sb.tile([P, PACK, M], F32, name="u_raw")
         x_codes = sb.tile([P, N], U32, name="x_codes", align_bytes=64)
         x_scales = sb.tile([P, N], U8, name="x_scales", align_bytes=64)
-        w_codes = sb.tile([P, M], U32, name="w_codes", align_bytes=64)
-        w_scales = sb.tile([P, M], U8, name="w_scales", align_bytes=64)
+        w_codes = sb.tile([P, N], U32, name="w_codes", align_bytes=64)
+        w_scales = sb.tile([P, N], U8, name="w_scales", align_bytes=64)
         u_codes = sb.tile([P, M], U32, name="u_codes", align_bytes=64)
         u_scales = sb.tile([P, M], U8, name="u_scales", align_bytes=64)
 
@@ -46,23 +46,25 @@ def tile_rows_gglu_relu_bias_kernel(tc, x, w, u, b, out):
             out=bias_rows[0:P:32, :].rearrange("q (g j) -> q g j", j=32),
             in_=b.rearrange("g (q j) o -> q g (j o)", j=32),
         )
-        x_raw = [sb.tile([P, PACK, N // 2], F32, name="x_raw%d" % h) for h in range(2)]
-        nc.sync.dma_start(out=x_raw[0][:], in_=x_rows[:, :, : N // 2])
-        nc.sync.dma_start(out=x_raw[1][:], in_=x_rows[:, :, N // 2 :])
+        x_raw = sb.tile([P, PACK, N], F32, name="x_raw")
         nc.sync.dma_start(out=w_raw[:], in_=w_rows)
+        nc.sync.dma_start(out=x_raw[:], in_=x_rows)
         nc.sync.dma_start(out=u_raw[:], in_=u_rows)
 
         def x_unit(i):
-            return x_raw[i // 2][:, :, (i % 2) * UNIT : (i % 2 + 1) * UNIT]
+            return x_raw[:, :, i * UNIT : (i + 1) * UNIT]
 
         raw = {"w": w_raw[:], "u": u_raw[:]}
-        codes = {"w": w_codes[:], "u": u_codes[:]}
-        scales = {"w": w_scales[:], "u": u_scales[:]}
+        codes = {"w": w_codes[:, :M], "u": u_codes[:]}
+        scales = {"w": w_scales[:, :M], "u": u_scales[:]}
         for i in range(N // UNIT):
             raw["x%d" % i] = x_unit(i)
             codes["x%d" % i] = x_codes[:, i * UNIT : (i + 1) * UNIT]
             scales["x%d" % i] = x_scales[:, i * UNIT : (i + 1) * UNIT]
         packed = {}
+        banks = {
+            name: [ps.tile([M, N], F32, name="%s%d" % (name, g)) for g in range(G)] for name in ("z", "gate")
+        }
 
         def interleave(key, copy):
             packed[key] = sb.tile([P, UNIT, PACK], BF16, name="packed_" + key, align_bytes=64)
@@ -78,33 +80,43 @@ def tile_rows_gglu_relu_bias_kernel(tc, x, w, u, b, out):
                 in_=packed[key][:].rearrange("p n t -> p (n t)"),
             )
 
-        def product(g, name, w_c, w_s):
+        def product(g, name, w_c, w_s, x_c=x_codes, x_s=x_scales):
             rows = slice(g * ROWS, (g + 1) * ROWS)
-            acc = ps.tile([M, N], F32, name="%s%d" % (name, g))
+            acc = banks[name][g]
             nc.tensor.matmul_mx(
                 out=acc[:],
-                lhsT=w_c[rows, :].bitcast(FP8X4),
-                lhsT_scale=w_s[rows, :],
-                rhs=x_codes[rows, :].bitcast(FP8X4),
-                rhs_scale=x_scales[rows, :],
+                lhsT=w_c[rows, :M].bitcast(FP8X4),
+                lhsT_scale=w_s[rows, :M],
+                rhs=x_c[rows, :].bitcast(FP8X4),
+                rhs_scale=x_s[rows, :],
                 start=True,
                 stop=True,
             )
             return acc
 
+        interleave("w", nc.vector.tensor_copy)
+        quantize("w")
+        for c in range(1, N // M):
+            cols = slice(c * M, (c + 1) * M)
+            nc.vector.quantize_mx(
+                out=w_codes[:, cols].bitcast(FP8X4),
+                scales=w_scales[:, cols],
+                in_=packed["w"][:].rearrange("p n t -> p (n t)"),
+            )
+        for r in range(4):
+            for g in range(G):
+                product(g, ("z", "gate")[r % 2], w_codes, w_scales, w_codes, w_scales)
         interleave("x0", nc.vector.tensor_copy)
-        interleave("x1", nc.scalar.copy)
+        interleave("x2", nc.scalar.copy)
+        interleave("x1", nc.vector.tensor_copy)
+        interleave("x3", nc.scalar.copy)
         quantize("x0")
         quantize("x1")
-        interleave("x2", nc.vector.tensor_copy)
-        interleave("x3", nc.scalar.copy)
-        interleave("w", nc.vector.tensor_copy)
+        interleave("u", nc.vector.tensor_copy)
         quantize("x2")
         quantize("x3")
-        quantize("w")
-        interleave("u", nc.scalar.copy)
-        nc.vector.transpose(out=bias_cols[:], in_=bias_rows[:])
         quantize("u")
+        nc.vector.transpose(out=bias_cols[:], in_=bias_rows[:])
 
         z, gate = {}, {}
         z[0] = product(0, "z", w_codes, w_scales)
@@ -117,12 +129,15 @@ def tile_rows_gglu_relu_bias_kernel(tc, x, w, u, b, out):
         gate[3] = product(3, "gate", u_codes, u_scales)
         half = N // 2
         for g in range(G):
+            res = sb.tile([M, N], F32, name="res%d" % g)
             for k in range(2):
                 cols = slice(k * half, (k + 1) * half)
                 act = sb.tile([M, half], F32, name="act%d_%d" % (g, k))
                 nc.scalar.activation(
                     out=act[:], in_=z[g][:, cols], func=RELU, bias=bias_cols[:, 32 * g : 32 * g + 1]
                 )
-                res = sb.tile([M, half], F32, name="res%d_%d" % (g, k))
-                nc.vector.tensor_tensor(out=res[:], in0=gate[g][:, cols], in1=act[:], op=MULT)
-                nc.sync.dma_start(out=out[g][:, cols], in_=res[:])
+                nc.vector.tensor_tensor(out=res[:, cols], in0=gate[g][:, cols], in1=act[:], op=MULT)
+                if g == 0:
+                    nc.sync.dma_start(out=out[g][:, cols], in_=res[:, cols])
+            if g > 0:
+                nc.sync.dma_start(out=out[g], in_=res[:])

@@ -46,13 +46,14 @@ def tile_rows_gglu_relu_bias_kernel(tc, x, w, u, b, out):
             out=bias_rows[0:P:32, :].rearrange("q (g j) -> q g j", j=32),
             in_=b.rearrange("g (q j) o -> q g (j o)", j=32),
         )
-        x_raw = sb.tile([P, PACK, N], F32, name="x_raw")
+        x_raw = [sb.tile([P, PACK, N // 2], F32, name="x_raw%d" % h) for h in range(2)]
         nc.sync.dma_start(out=w_raw[:], in_=w_rows)
-        nc.sync.dma_start(out=x_raw[:], in_=x_rows)
+        nc.sync.dma_start(out=x_raw[0][:], in_=x_rows[:, :, : N // 2])
+        nc.sync.dma_start(out=x_raw[1][:], in_=x_rows[:, :, N // 2 :])
         nc.sync.dma_start(out=u_raw[:], in_=u_rows)
 
         def x_unit(i):
-            return x_raw[:, :, i * UNIT : (i + 1) * UNIT]
+            return x_raw[i // 2][:, :, (i % 2) * UNIT : (i % 2 + 1) * UNIT]
 
         raw = {"w": w_raw[:], "u": u_raw[:]}
         codes = {"w": w_codes[:, :M], "u": u_codes[:]}
@@ -103,20 +104,20 @@ def tile_rows_gglu_relu_bias_kernel(tc, x, w, u, b, out):
                 scales=w_scales[:, cols],
                 in_=packed["w"][:].rearrange("p n t -> p (n t)"),
             )
-        for r in range(4):
+        for r in range(3):
             for g in range(G):
                 product(g, ("z", "gate")[r % 2], w_codes, w_scales, w_codes, w_scales)
         interleave("x0", nc.vector.tensor_copy)
-        interleave("x2", nc.scalar.copy)
-        interleave("x1", nc.vector.tensor_copy)
-        interleave("x3", nc.scalar.copy)
+        interleave("x1", nc.scalar.copy)
         quantize("x0")
         quantize("x1")
-        interleave("u", nc.vector.tensor_copy)
+        interleave("x2", nc.vector.tensor_copy)
+        interleave("x3", nc.scalar.copy)
+        interleave("u", nc.scalar.copy)
         quantize("x2")
         quantize("x3")
-        quantize("u")
         nc.vector.transpose(out=bias_cols[:], in_=bias_rows[:])
+        quantize("u")
 
         z, gate = {}, {}
         z[0] = product(0, "z", w_codes, w_scales)

from contextlib import ExitStack

import concourse.mybir as mybir

G, D, M, N = 4, 128, 128, 512
FLOPS = 2 * 2 * G * D * M * N

F32 = mybir.dt.float32
BF16 = mybir.dt.bfloat16
U32 = mybir.dt.uint32
U8 = mybir.dt.uint8
FP8X4 = mybir.dt.float8_e4m3fn_x4
RELU = mybir.ActivationFunctionType.Relu
MULT = mybir.AluOpType.mult

P = 128
PACK = 4
ROWS = D // PACK
UNIT = 128


def tile_rows_gglu_relu_bias_kernel(tc, x, w, u, b, out):
    nc = tc.nc
    with ExitStack() as ctx:
        sb = ctx.enter_context(tc.tile_pool(name="sb", bufs=1))
        ps = ctx.enter_context(tc.psum_pool(name="ps", bufs=1))
        ctx.enter_context(tc.manual_schedule())

        x_rows = x.rearrange("g (p j) n -> (g p) j n", j=PACK)
        w_rows = w.rearrange("g (p j) m -> (g p) j m", j=PACK)
        u_rows = u.rearrange("g (p j) m -> (g p) j m", j=PACK)

        bias_rows = sb.tile([P, P], F32, name="bias_rows", align_bytes=64)
        bias_cols = sb.tile([P, P], F32, name="bias_cols", align_bytes=64)
        w_raw = sb.tile([P, PACK, M], F32, name="w_raw")
        u_raw = sb.tile([P, PACK, M], F32, name="u_raw")
        x_codes = sb.tile([P, N], U32, name="x_codes", align_bytes=64)
        x_scales = sb.tile([P, N], U8, name="x_scales", align_bytes=64)
        w_codes = sb.tile([P, N], U32, name="w_codes", align_bytes=64)
        w_scales = sb.tile([P, N], U8, name="w_scales", align_bytes=64)
        u_codes = sb.tile([P, M], U32, name="u_codes", align_bytes=64)
        u_scales = sb.tile([P, M], U8, name="u_scales", align_bytes=64)

        nc.vector.memset(bias_rows[:], 0.0)
        nc.scalar.dma_start(
            out=bias_rows[0:P:32, :].rearrange("q (g j) -> q g j", j=32),
            in_=b.rearrange("g (q j) o -> q g (j o)", j=32),
        )
        x_raw = [sb.tile([P, PACK, N // 2], F32, name="x_raw%d" % h) for h in range(2)]
        nc.sync.dma_start(out=w_raw[:], in_=w_rows)
        nc.sync.dma_start(out=x_raw[0][:], in_=x_rows[:, :, : N // 2])
        nc.sync.dma_start(out=x_raw[1][:], in_=x_rows[:, :, N // 2 :])
        nc.sync.dma_start(out=u_raw[:], in_=u_rows)

        def x_unit(i):
            return x_raw[i // 2][:, :, (i % 2) * UNIT : (i % 2 + 1) * UNIT]

        raw = {"w": w_raw[:], "u": u_raw[:]}
        codes = {"w": w_codes[:, :M], "u": u_codes[:]}
        scales = {"w": w_scales[:, :M], "u": u_scales[:]}
        for i in range(N // UNIT):
            raw["x%d" % i] = x_unit(i)
            codes["x%d" % i] = x_codes[:, i * UNIT : (i + 1) * UNIT]
            scales["x%d" % i] = x_scales[:, i * UNIT : (i + 1) * UNIT]
        packed = {}
        banks = {
            name: [ps.tile([M, N], F32, name="%s%d" % (name, g)) for g in range(G)] for name in ("z", "gate")
        }

        def interleave(key, copy):
            packed[key] = sb.tile([P, UNIT, PACK], BF16, name="packed_" + key, align_bytes=64)
            copy(
                out=packed[key][:].rearrange("p (c i) t -> p c t i", i=4),
                in_=raw[key].rearrange("p t (c i) -> p c t i", i=4),
            )

        def quantize(key):
            nc.vector.quantize_mx(
                out=codes[key].bitcast(FP8X4),
                scales=scales[key],
                in_=packed[key][:].rearrange("p n t -> p (n t)"),
            )

        def product(g, name, w_c, w_s, x_c=x_codes, x_s=x_scales):
            rows = slice(g * ROWS, (g + 1) * ROWS)
            acc = banks[name][g]
            nc.tensor.matmul_mx(
                out=acc[:],
                lhsT=w_c[rows, :M].bitcast(FP8X4),
                lhsT_scale=w_s[rows, :M],
                rhs=x_c[rows, :].bitcast(FP8X4),
                rhs_scale=x_s[rows, :],
                start=True,
                stop=True,
            )
            return acc

        interleave("w", nc.vector.tensor_copy)
        quantize("w")
        for c in range(1, N // M):
            cols = slice(c * M, (c + 1) * M)
            nc.vector.quantize_mx(
                out=w_codes[:, cols].bitcast(FP8X4),
                scales=w_scales[:, cols],
                in_=packed["w"][:].rearrange("p n t -> p (n t)"),
            )
        for r in range(3):
            for g in range(G):
                product(g, ("z", "gate")[r % 2], w_codes, w_scales, w_codes, w_scales)
        interleave("x0", nc.vector.tensor_copy)
        interleave("x1", nc.scalar.copy)
        quantize("x0")
        quantize("x1")
        interleave("x2", nc.vector.tensor_copy)
        interleave("x3", nc.scalar.copy)
        interleave("u", nc.scalar.copy)
        quantize("x2")
        quantize("x3")
        nc.vector.transpose(out=bias_cols[:], in_=bias_rows[:])
        quantize("u")

        z, gate = {}, {}
        z[0] = product(0, "z", w_codes, w_scales)
        z[1] = product(1, "z", w_codes, w_scales)
        gate[0] = product(0, "gate", u_codes, u_scales)
        z[2] = product(2, "z", w_codes, w_scales)
        gate[1] = product(1, "gate", u_codes, u_scales)
        z[3] = product(3, "z", w_codes, w_scales)
        gate[2] = product(2, "gate", u_codes, u_scales)
        gate[3] = product(3, "gate", u_codes, u_scales)
        half = N // 2
        for g in range(G):
            res = sb.tile([M, N], F32, name="res%d" % g)
            for k in range(2):
                cols = slice(k * half, (k + 1) * half)
                act = sb.tile([M, half], F32, name="act%d_%d" % (g, k))
                nc.scalar.activation(
                    out=act[:], in_=z[g][:, cols], func=RELU, bias=bias_cols[:, 32 * g : 32 * g + 1]
                )
                nc.vector.tensor_tensor(out=res[:, cols], in0=gate[g][:, cols], in1=act[:], op=MULT)
                if g == 0:
                    nc.sync.dma_start(out=out[g][:, cols], in_=res[:, cols])
            if g > 0:
                nc.sync.dma_start(out=out[g], in_=res[:])
